import numpy as np
import ml_dtypes


def mxq(x, axis, fmt="e4m3"):
    dtype, down = {"e4m3": (ml_dtypes.float8_e4m3fn, 7), "e5m2": (ml_dtypes.float8_e5m2, 14)}[fmt]
    v = np.moveaxis(np.asarray(x, np.float32).astype(ml_dtypes.bfloat16).astype(np.float64), axis, -1)
    blocks = v.reshape(v.shape[:-1] + (-1, 32))
    amax = np.abs(blocks).max(-1, keepdims=True)
    byte = np.maximum(np.where(amax > 0, np.frexp(amax)[1] - 1 + 127, 0) - down, 1)
    scale = np.exp2(byte - 127.0)
    codes = (blocks / scale).astype(np.float32).astype(dtype).astype(np.float64)
    return np.moveaxis((codes * scale).reshape(v.shape), -1, axis)


WIDE = False


def mx_kscale(k):
    if not WIDE:
        return np.ones(k)
    levels = np.array([30, -30])
    if k % 512:
        return np.exp2(np.random.permutation(np.resize(levels, k // 32))).repeat(32)
    a = np.empty((k // 512, 16))
    for p in range(k // 512):
        a[p, :8] = np.random.permutation(np.resize(levels, 8))
        for g in range(8):
            far = levels[np.abs(levels - a[p, g]) >= 10]
            a[p, g + 8] = far[np.random.randint(len(far))]
    return np.exp2(a.ravel()).repeat(32)


def f64(x):
    return np.asarray(x).astype(np.float64)


def striped(idx):
    return np.tile(np.asarray(idx).reshape(-1, 16).T, (8, 1)).astype(np.uint16)


def unstriped(offs):
    return offs[:16].T.reshape(-1).astype(np.int64)


E2M1 = np.array([0.0, 0.5, 1.0, 1.5, 2.0, 3.0, 4.0, 6.0, -0.0, -0.5, -1.0, -1.5, -2.0, -3.0, -4.0, -6.0])


def pack_weight(w, fmt):
    k, n = w.shape
    w = f64(np.asarray(w, np.float32).astype(ml_dtypes.bfloat16)).reshape(k // 32, 32, n)
    amax = np.abs(w).max(1)
    if fmt in ("e4m3", "e5m2"):
        byte = np.frexp(amax)[1] - 1 + 127 - (7 if fmt == "e4m3" else 14)
    else:
        mant, ex = np.frexp(amax / 6.0)
        byte = np.where(mant > 0.5, ex, ex - 1) + 127
    byte = np.clip(np.where(amax > 0, byte, 1), 1, 254)
    scaled = (w * np.exp2(127.0 - byte)[:, None, :]).reshape(k, n).astype(np.float32)
    by_word = np.ascontiguousarray(scaled.reshape(k // 512, 128, 4, n).transpose(0, 1, 3, 2))
    if fmt in ("e4m3", "e5m2"):
        words = by_word.astype(ml_dtypes.float8_e4m3fn if fmt == "e4m3" else ml_dtypes.float8_e5m2).view(np.uint8)
    else:
        c = by_word.astype(ml_dtypes.float4_e2m1fn).view(np.uint8) & 0xF
        words = (c[..., 0::2] | (c[..., 1::2] << 4)).reshape(k // 512, 128, 2 * n)
    return np.ascontiguousarray(words), np.ascontiguousarray(byte.astype(np.uint8).reshape(k // 512, 16, n))


def unpack_weight(words, scales, fmt):
    g, _, n = scales.shape
    words = np.ascontiguousarray(words).reshape(g, 128, n, -1)
    if fmt in ("e4m3", "e5m2"):
        vals = words.view(ml_dtypes.float8_e4m3fn if fmt == "e4m3" else ml_dtypes.float8_e5m2).astype(np.float64)
    else:
        nib = np.empty((g, 128, n, 4), np.uint8)
        nib[..., 0::2] = words & 0xF
        nib[..., 1::2] = words >> 4
        vals = E2M1[nib]
    vals = vals * np.repeat(np.exp2(scales.astype(np.float64) - 127.0), 8, axis=1)[..., None]
    return vals.transpose(0, 1, 3, 2).reshape(g * 512, n)


K, F, T, Z, J, R, V, O, N = 512, 512, 1024, 1024, 256, 512, 1024, 128, 256


def setup_inputs():
    n = np.random.standard_normal
    idx = np.random.permutation(T)[:J]
    idx2 = np.random.permutation(Z)[:J]
    idx3 = np.random.permutation(V)[:O]
    idx4 = np.random.permutation(J)[:O]
    idx5 = np.random.permutation(T)[:O]
    fk = mx_kscale(K)
    fr = mx_kscale(R)
    ff = mx_kscale(F)
    xtp = pack_weight(n((K, T)) / fk[:, None], "e2m1")
    wp = pack_weight(n((K, R)) * 1 / np.sqrt(K) * fk[:, None] * fr, "e5m2")
    xop = pack_weight(n((F, Z)) / ff[:, None], "e5m2")
    w0p = pack_weight(n((F, R)) * 1 / np.sqrt(F) * ff[:, None] * fr, "e4m3")
    wbp = pack_weight(n((R, N)) * 1 / np.sqrt(R) / fr[:, None], "e4m3")
    wsp = pack_weight(n((K, N)) * 1 / np.sqrt(K) * fk[:, None], "e4m3")
    return {
        "xt_words": xtp[0],
        "xt_scales": xtp[1],
        "w_words": wp[0],
        "w_scales": wp[1],
        "xo_words": xop[0],
        "xo_scales": xop[1],
        "w0_words": w0p[0],
        "w0_scales": w0p[1],
        "tb": (np.random.randint(-9, 10, (R, V)).astype(np.float64)).astype(np.float32),
        "st": (np.random.uniform(0.12, 0.3, (R, 1)) * fr[:, None]).astype(np.float32),
        "sa": (np.random.uniform(0.5, 1.6, (R, 1))).astype(np.float32),
        "wb_words": wbp[0],
        "wb_scales": wbp[1],
        "ws_words": wsp[0],
        "ws_scales": wsp[1],
        "offs": striped(idx),
        "offs2": striped(idx2),
        "offs3": striped(idx3),
        "offs4": striped(idx4),
        "offs5": striped(idx5),
    }


def reference(xt_words, xt_scales, w_words, w_scales, xo_words, xo_scales, w0_words, w0_scales, tb, st, sa, wb_words, wb_scales, ws_words, ws_scales, offs, offs2, offs3, offs4, offs5):
    idx = unstriped(offs)
    idx2 = unstriped(offs2)
    idx3 = unstriped(offs3)
    idx4 = unstriped(offs4)
    idx5 = unstriped(offs5)
    xtu = unpack_weight(xt_words, xt_scales, "e2m1")
    wu = unpack_weight(w_words, w_scales, "e5m2")
    xou = unpack_weight(xo_words, xo_scales, "e5m2")
    w0u = unpack_weight(w0_words, w0_scales, "e4m3")
    wbu = unpack_weight(wb_words, wb_scales, "e4m3")
    wsu = unpack_weight(ws_words, ws_scales, "e4m3")
    xtidxg = xtu[:, idx]
    xoidx2g = xou[:, idx2]
    a = wu.T @ xtidxg + w0u.T @ xoidx2g
    hid = np.abs(f64(tb)[:, idx3] * f64(st) - a[:, idx4] * f64(sa))
    hidq = mxq(hid, 0, "e5m2")
    xtidx5g = xtu[:, idx5]
    y = wbu.T @ hidq + wsu.T @ xtidx5g
    return y

@@ -1,0 +1,187 @@
+from contextlib import ExitStack
+
+import concourse.mybir as mybir
+
+K, F, T, Z, J, R, V, O, N = 512, 512, 1024, 1024, 256, 512, 1024, 128, 256
+FLOPS = 2 * (K * R * J + F * R * J + R * N * O + K * N * O)
+
+F32 = mybir.dt.float32
+BF16 = mybir.dt.bfloat16
+I32 = mybir.dt.int32
+U32 = mybir.dt.uint32
+U16 = mybir.dt.uint16
+U8 = mybir.dt.uint8
+E4M3 = mybir.dt.float8_e4m3fn_x4
+E5M2 = mybir.dt.float8_e5m2_x4
+E2M1 = mybir.dt.float4_e2m1fn_x4
+ALU = mybir.AluOpType
+COPY = mybir.ActivationFunctionType.Copy
+
+P = 128
+PACK = 4
+QUAD = 32
+
+
+def tile_list_tableread_bank_further_plain_kernel(
+    tc, xt_words, xt_scales, w_words, w_scales, xo_words, xo_scales, w0_words, w0_scales, tb, st, sa,
+    wb_words, wb_scales, ws_words, ws_scales, offs, offs2, offs3, offs4, offs5, out,
+):
+    nc = tc.nc
+    with ExitStack() as ctx:
+        sb = ctx.enter_context(tc.tile_pool(name="sb", bufs=1))
+        ps = ctx.enter_context(tc.psum_pool(name="ps", bufs=1))
+
+        def tile(name, shape, dtype):
+            return sb.tile(shape, dtype, name=name, align_bytes=64)
+
+        def load_list(name, src):
+            lst = tile(name, list(src.shape), U16)
+            nc.sync.dma_start(lst[:], src)
+            return lst
+
+        def load_words(name, src, columns):
+            words = tile(name, [P, columns], U32)
+            nc.sync.dma_start(words[:].bitcast(I32), src[0].rearrange("p n t -> p (n t)").bitcast(I32))
+            return words
+
+        def zeroed(name, shape):
+            plane = tile(name, shape, U8)
+            nc.vector.memset(plane[:].bitcast(I32), 0)
+            return plane
+
+        def load_plane_direct(queue, plane, src):
+            rows = src[0].bitcast(I32)
+            for q in range(4):
+                queue.dma_start(plane[QUAD * q : QUAD * q + 4, :].bitcast(I32), rows[4 * q : 4 * q + 4, :])
+
+        def load_plane_halves(queue, plane, src):
+            rows = src[0].bitcast(I32).rearrange("(h q r) n -> q r h n", h=2, q=2)
+            for q in range(2):
+                queue.dma_start(plane[QUAD * q : QUAD * q + 4, :, :].bitcast(I32), rows[q])
+
+        def lift_upper_half(plane):
+            nc.vector.tensor_copy(plane[64:128, 0, :].bitcast(I32), plane[0:64, 1, :].bitcast(I32))
+
+        def load_staged(queue, staged, src):
+            queue.dma_start(staged.bitcast(I32), src[0].bitcast(I32).rearrange("(q r) n -> r q n", r=4))
+
+        def spread(plane, staged):
+            for q in range(4):
+                nc.vector.tensor_copy(plane[QUAD * q : QUAD * q + 4, :].bitcast(I32), staged[:, q, :].bitcast(I32))
+
+        def gather(name, window, lst, n):
+            got = tile(name, [P, n], window.dtype)
+            nc.vector.tensor_copy(got[:], window[:].indirect(lst[:]))
+            return got
+
+
+        def deal_words(name, words):
+            dealt = tile(name, [P, R], U32)
+            nc.scalar.copy(dealt[:].rearrange("p (t m) -> p m t", t=PACK), words[:].rearrange("p (m t) -> p m t", t=PACK))
+            return dealt
+
+        def deal_scales(name, plane):
+            dealt = tile(name, [P, R], U8)
+            nc.vector.tensor_copy(dealt[:].rearrange("p (t m) -> p t m", t=PACK), plane.rearrange("p (m t) -> p t m", t=PACK))
+            return dealt
+
+        xt_s = zeroed("xt_s", [P, T])
+        xo_s = zeroed("xo_s", [P, Z])
+        w_s = zeroed("w_s", [P, R])
+        w0_s = zeroed("w0_s", [P, R])
+        out_sc = zeroed("out_sc", [P, 2 * N])
+
+        def staged_rows(name, src, n):
+            staged = tile(name, [4, 4, n], U8)
+            load_staged(nc.scalar, staged[:], src)
+            return staged
+
+        l1 = load_list("l1", offs)
+        xt_st = staged_rows("xt_st", xt_scales, T)
+        xt_w = tile("xt_w", [P, T], U16)
+        nc.sync.dma_start(xt_w[:].bitcast(I32), xt_words[0].bitcast(I32))
+        w_st = staged_rows("w_st", w_scales, R)
+        w_w = load_words("w_w", w_words, R)
+        xo_st = staged_rows("xo_st", xo_scales, Z)
+        l2 = load_list("l2", offs2)
+        w0_st = staged_rows("w0_st", w0_scales, R)
+        xo_w = load_words("xo_w", xo_words, Z)
+        w0_w = load_words("w0_w", w0_words, R)
+        st_sb = tile("st_sb", [P, PACK], F32)
+        sa_sb = tile("sa_sb", [P, PACK], F32)
+        nc.scalar.dma_start(st_sb[:], st.rearrange("(p t) o -> p (t o)", t=PACK))
+        nc.scalar.dma_start(sa_sb[:], sa.rearrange("(p t) o -> p (t o)", t=PACK))
+        out_staged = tile("out_staged", [4, 4, 2 * N], U8)
+        load_staged(nc.scalar, out_staged[:, :, 0:N], wb_scales)
+        load_staged(nc.scalar, out_staged[:, :, N : 2 * N], ws_scales)
+        tb_rows = tb.rearrange("(p t) v -> t p v", t=PACK)
+        tb_sb = [tile(f"tb_sb{t}", [P, V], F32) for t in range(PACK)]
+        l3 = load_list("l3", offs3)
+        nc.sync.dma_start(tb_sb[0][:], tb_rows[0])
+        l4 = load_list("l4", offs4)
+        l5 = load_list("l5", offs5)
+        nc.sync.dma_start(tb_sb[1][:], tb_rows[1])
+        nc.sync.dma_start(tb_sb[2][:], tb_rows[2])
+        nc.sync.dma_start(tb_sb[3][:], tb_rows[3])
+        ws_w = load_words("ws_w", ws_words, N)
+        wb_w = load_words("wb_w", wb_words, N)
+
+        spread(xt_s, xt_st)
+        xt_g = gather("xt_g", xt_w, l1, J)
+        xt_gs = gather("xt_gs", xt_s, l1, J)
+        w_dealt = deal_words("w_dealt", w_w)
+        spread(w_s, w_st)
+        w_sc = deal_scales("w_sc", w_s[:])
+        spread(xo_s, xo_st)
+        spread(w0_s, w0_st)
+        w0_sc = deal_scales("w0_sc", w0_s[:])
+        xo_gs = gather("xo_gs", xo_s, l2, J)
+        xo_g = gather("xo_g", xo_w, l2, J)
+        w0_dealt = deal_words("w0_dealt", w0_w)
+
+        a_ps = [ps.tile([P, J], F32, name=f"a_ps{t}") for t in range(PACK)]
+        for t in range(PACK):
+            cols = slice(P * t, P * (t + 1))
+            nc.tensor.matmul_mx(out=a_ps[t][:], lhsT=w_dealt[:, cols].bitcast(E5M2), lhsT_scale=w_sc[:, cols],
+                                rhs=xt_g[:].bitcast(E2M1), rhs_scale=xt_gs[:], start=True, stop=False)
+        for t in range(PACK):
+            cols = slice(P * t, P * (t + 1))
+            nc.tensor.matmul_mx(out=a_ps[t][:], lhsT=w0_dealt[:, cols].bitcast(E4M3), lhsT_scale=w0_sc[:, cols],
+                                rhs=xo_g[:].bitcast(E5M2), rhs_scale=xo_gs[:], start=False, stop=True)
+
+        levels = tile("levels", [P, PACK, O], F32)
+        picked = tile("picked", [P, PACK, O], F32)
+        diff = tile("diff", [P, PACK, O], F32)
+        hid = tile("hid", [P, O, PACK], BF16)
+        for t in range(PACK):
+            a_sb = tile(f"a_sb{t}", [P, J], F32)
+            nc.vector.tensor_copy(a_sb[:], a_ps[t][:])
+            nc.scalar.activation(levels[:, t, :], tb_sb[t][:].indirect(l3[:]), COPY, scale=st_sb[:, t : t + 1])
+            nc.scalar.activation(picked[:, t, :], a_sb[:].indirect(l4[:]), COPY, scale=sa_sb[:, t : t + 1])
+
+        xt_g5 = gather("xt_g5", xt_w, l5, O)
+        xt_gs5 = gather("xt_gs5", xt_s, l5, O)
+        spread(out_sc, out_staged)
+        y_ps = [ps.tile([P, O], F32, name=f"y_ps{h}") for h in range(2)]
+        for h in range(2):
+            nc.tensor.matmul_mx(out=y_ps[h][:], lhsT=ws_w[:, P * h : P * (h + 1)].bitcast(E4M3),
+                                lhsT_scale=out_sc[:, N + P * h : N + P * (h + 1)],
+                                rhs=xt_g5[:].bitcast(E2M1), rhs_scale=xt_gs5[:], start=True, stop=False)
+
+        for u in range(2):
+            for t in (2 * u, 2 * u + 1):
+                nc.vector.tensor_tensor(diff[:, t, :], levels[:, t, :], picked[:, t, :], ALU.subtract)
+            pair = diff[:, 2 * u : 2 * u + 2, :].rearrange("p t o -> p o t")
+            nc.vector.scalar_tensor_tensor(hid[:, :, 2 * u : 2 * u + 2], pair, -1.0, pair, ALU.mult, ALU.max)
+
+        hid_q = tile("hid_q", [P, O], U32)
+        hid_s = tile("hid_s", [P, O], U8)
+        nc.vector.quantize_mx(out=hid_q[:].bitcast(E5M2), scales=hid_s[:], in_=hid[:].rearrange("p o t -> p (o t)"))
+        y_sb = tile("y_sb", [P, 2, O], F32)
+        for h in range(2):
+            nc.tensor.matmul_mx(out=y_ps[h][:], lhsT=wb_w[:, P * h : P * (h + 1)].bitcast(E4M3),
+                                lhsT_scale=out_sc[:, P * h : P * (h + 1)],
+                                rhs=hid_q[:].bitcast(E5M2), rhs_scale=hid_s[:], start=False, stop=True)
+        nc.vector.tensor_copy(y_sb[:, 0, :], y_ps[0][:])
+        nc.scalar.copy(y_sb[:, 1, :], y_ps[1][:])
+        nc.sync.dma_start(out.rearrange("(h p) o -> p h o", h=2), y_sb[:])

@@ -16,6 +16,7 @@ E5M2 = mybir.dt.float8_e5m2_x4
 E2M1 = mybir.dt.float4_e2m1fn_x4
 ALU = mybir.AluOpType
 COPY = mybir.ActivationFunctionType.Copy
+ABS = mybir.ActivationFunctionType.Abs
 
 P = 128
 PACK = 4
@@ -85,94 +86,97 @@ def tile_list_tableread_bank_further_plain_kernel(
             nc.vector.tensor_copy(dealt[:].rearrange("p (t m) -> p t m", t=PACK), plane.rearrange("p (m t) -> p t m", t=PACK))
             return dealt
 
-        xt_s = zeroed("xt_s", [P, T])
-        xo_s = zeroed("xo_s", [P, Z])
-        w_s = zeroed("w_s", [P, R])
-        w0_s = zeroed("w0_s", [P, R])
-        out_sc = zeroed("out_sc", [P, 2 * N])
+        def halves(queue, plane, src):
+            rows = src[0].bitcast(I32).rearrange("(h q r) n -> q r h n", h=2, q=2)
+            for q in range(2):
+                queue.dma_start(plane[QUAD * q : QUAD * q + 4].bitcast(I32), rows[q])
 
-        def staged_rows(name, src, n):
-            staged = tile(name, [4, 4, n], U8)
-            load_staged(nc.scalar, staged[:], src)
-            return staged
-
-        l1 = load_list("l1", offs)
-        xt_st = staged_rows("xt_st", xt_scales, T)
+        xt_st = zeroed("xt_st", [64, 2, T])
+        xo_st = zeroed("xo_st", [64, 2, Z])
+        w_pl = zeroed("w_pl", [P, 2, 2 * R])
+        out_pl = zeroed("out_pl", [P, 2, 2 * N])
         xt_w = tile("xt_w", [P, T], U16)
-        nc.sync.dma_start(xt_w[:].bitcast(I32), xt_words[0].bitcast(I32))
-        w_st = staged_rows("w_st", w_scales, R)
-        w_w = load_words("w_w", w_words, R)
-        xo_st = staged_rows("xo_st", xo_scales, Z)
-        l2 = load_list("l2", offs2)
-        w0_st = staged_rows("w0_st", w0_scales, R)
-        xo_w = load_words("xo_w", xo_words, Z)
-        w0_w = load_words("w0_w", w0_words, R)
         st_sb = tile("st_sb", [P, PACK], F32)
         sa_sb = tile("sa_sb", [P, PACK], F32)
-        nc.scalar.dma_start(st_sb[:], st.rearrange("(p t) o -> p (t o)", t=PACK))
-        nc.scalar.dma_start(sa_sb[:], sa.rearrange("(p t) o -> p (t o)", t=PACK))
-        out_staged = tile("out_staged", [4, 4, 2 * N], U8)
-        load_staged(nc.scalar, out_staged[:, :, 0:N], wb_scales)
-        load_staged(nc.scalar, out_staged[:, :, N : 2 * N], ws_scales)
         tb_rows = tb.rearrange("(p t) v -> t p v", t=PACK)
         tb_sb = [tile(f"tb_sb{t}", [P, V], F32) for t in range(PACK)]
-        l3 = load_list("l3", offs3)
+
+        l1 = load_list("l1", offs)
+        nc.sync.dma_start(xt_w[:].bitcast(I32), xt_words[0].bitcast(I32))
+        halves(nc.sync, xt_st[:], xt_scales)
+        halves(nc.sync, xo_st[:], xo_scales)
+        l2 = load_list("l2", offs2)
+        xo_w = load_words("xo_w", xo_words, Z)
+        w_w = load_words("w_w", w_words, R)
+        w0_w = load_words("w0_w", w0_words, R)
+        halves(nc.sync, w_pl[:, :, 0:R], w_scales)
+        halves(nc.sync, w_pl[:, :, R : 2 * R], w0_scales)
         nc.sync.dma_start(tb_sb[0][:], tb_rows[0])
-        l4 = load_list("l4", offs4)
-        l5 = load_list("l5", offs5)
+        l3 = load_list("l3", offs3)
+        nc.sync.dma_start(st_sb[:], st.rearrange("(p t) o -> p (t o)", t=PACK))
         nc.sync.dma_start(tb_sb[1][:], tb_rows[1])
+        l4 = load_list("l4", offs4)
+        nc.sync.dma_start(sa_sb[:], sa.rearrange("(p t) o -> p (t o)", t=PACK))
+        l5 = load_list("l5", offs5)
         nc.sync.dma_start(tb_sb[2][:], tb_rows[2])
+        halves(nc.sync, out_pl[:, :, 0:N], wb_scales)
+        halves(nc.sync, out_pl[:, :, N : 2 * N], ws_scales)
         nc.sync.dma_start(tb_sb[3][:], tb_rows[3])
         ws_w = load_words("ws_w", ws_words, N)
         wb_w = load_words("wb_w", wb_words, N)
 
-        spread(xt_s, xt_st)
+        xt_s = tile("xt_s", [P, T], U8)
+        xo_s = tile("xo_s", [P, Z], U8)
+        for h in range(2):
+            for plane, staged in ((xt_s, xt_st), (xo_s, xo_st)):
+                nc.vector.tensor_copy(plane[64 * h : 64 * h + 64, :].bitcast(I32), staged[:, h, :].bitcast(I32))
         xt_g = gather("xt_g", xt_w, l1, J)
         xt_gs = gather("xt_gs", xt_s, l1, J)
-        w_dealt = deal_words("w_dealt", w_w)
-        spread(w_s, w_st)
-        w_sc = deal_scales("w_sc", w_s[:])
-        spread(xo_s, xo_st)
-        spread(w0_s, w0_st)
-        w0_sc = deal_scales("w0_sc", w0_s[:])
         xo_gs = gather("xo_gs", xo_s, l2, J)
         xo_g = gather("xo_g", xo_w, l2, J)
+        w_dealt = deal_words("w_dealt", w_w)
         w0_dealt = deal_words("w0_dealt", w0_w)
-
+        lift_upper_half(w_pl)
+        by_slot = w_pl[:, 0, :].rearrange("p (x m t) -> p t x m", x=2, t=PACK)
         a_ps = [ps.tile([P, J], F32, name=f"a_ps{t}") for t in range(PACK)]
         for t in range(PACK):
+            sc = tile(f"sc{t}", [P, 2, P], U8)
+            nc.vector.tensor_copy(sc[:], by_slot[:, t])
             cols = slice(P * t, P * (t + 1))
-            nc.tensor.matmul_mx(out=a_ps[t][:], lhsT=w_dealt[:, cols].bitcast(E5M2), lhsT_scale=w_sc[:, cols],
+            nc.tensor.matmul_mx(out=a_ps[t][:], lhsT=w_dealt[:, cols].bitcast(E5M2), lhsT_scale=sc[:, 0, :],
                                 rhs=xt_g[:].bitcast(E2M1), rhs_scale=xt_gs[:], start=True, stop=False)
-        for t in range(PACK):
-            cols = slice(P * t, P * (t + 1))
-            nc.tensor.matmul_mx(out=a_ps[t][:], lhsT=w0_dealt[:, cols].bitcast(E4M3), lhsT_scale=w0_sc[:, cols],
+            nc.tensor.matmul_mx(out=a_ps[t][:], lhsT=w0_dealt[:, cols].bitcast(E4M3), lhsT_scale=sc[:, 1, :],
                                 rhs=xo_g[:].bitcast(E5M2), rhs_scale=xo_gs[:], start=False, stop=True)
 
         levels = tile("levels", [P, PACK, O], F32)
-        picked = tile("picked", [P, PACK, O], F32)
         diff = tile("diff", [P, PACK, O], F32)
         hid = tile("hid", [P, O, PACK], BF16)
         for t in range(PACK):
+            nc.scalar.activation(levels[:, t, :], tb_sb[t][:].indirect(l3[:]), COPY, scale=st_sb[:, t : t + 1])
+        picked_first = sb.tile([P, PACK - 1, O], F32, name="picked_first", tag="tb_sb1", align_bytes=64)
+        picked_last = sb.tile([P, O], F32, name="picked_last", tag="tb_sb2", align_bytes=64)
+        picked = [picked_first[:, t, :] for t in range(PACK - 1)] + [picked_last[:]]
+        for t in range(PACK):
             a_sb = tile(f"a_sb{t}", [P, J], F32)
             nc.vector.tensor_copy(a_sb[:], a_ps[t][:])
-            nc.scalar.activation(levels[:, t, :], tb_sb[t][:].indirect(l3[:]), COPY, scale=st_sb[:, t : t + 1])
-            nc.scalar.activation(picked[:, t, :], a_sb[:].indirect(l4[:]), COPY, scale=sa_sb[:, t : t + 1])
+            nc.scalar.activation(picked[t], a_sb[:].indirect(l4[:]), COPY, scale=sa_sb[:, t : t + 1])
 
         xt_g5 = gather("xt_g5", xt_w, l5, O)
         xt_gs5 = gather("xt_gs5", xt_s, l5, O)
-        spread(out_sc, out_staged)
+        lift_upper_half(out_pl)
+        out_sc = out_pl[:, 0, :]
         y_ps = [ps.tile([P, O], F32, name=f"y_ps{h}") for h in range(2)]
         for h in range(2):
             nc.tensor.matmul_mx(out=y_ps[h][:], lhsT=ws_w[:, P * h : P * (h + 1)].bitcast(E4M3),
                                 lhsT_scale=out_sc[:, N + P * h : N + P * (h + 1)],
                                 rhs=xt_g5[:].bitcast(E2M1), rhs_scale=xt_gs5[:], start=True, stop=False)
 
-        for u in range(2):
-            for t in (2 * u, 2 * u + 1):
-                nc.vector.tensor_tensor(diff[:, t, :], levels[:, t, :], picked[:, t, :], ALU.subtract)
-            pair = diff[:, 2 * u : 2 * u + 2, :].rearrange("p t o -> p o t")
-            nc.vector.scalar_tensor_tensor(hid[:, :, 2 * u : 2 * u + 2], pair, -1.0, pair, ALU.mult, ALU.max)
+        nc.vector.tensor_tensor(diff[:, 0 : PACK - 1, :], levels[:, 0 : PACK - 1, :], picked_first[:], ALU.subtract)
+        nc.vector.tensor_tensor(diff[:, PACK - 1, :], levels[:, PACK - 1, :], picked_last[:], ALU.subtract)
+        woven = diff[:].rearrange("p t o -> p o t")
+        half = O // 2
+        nc.scalar.activation(hid[:, 0:half, :], woven[:, 0:half, :], ABS)
+        nc.vector.scalar_tensor_tensor(hid[:, half:O, :], woven[:, half:O, :], -1.0, woven[:, half:O, :], ALU.mult, ALU.max)
 
         hid_q = tile("hid_q", [P, O], U32)
         hid_s = tile("hid_s", [P, O], U8)

from contextlib import ExitStack

import concourse.mybir as mybir

K, F, T, Z, J, R, V, O, N = 512, 512, 1024, 1024, 256, 512, 1024, 128, 256
FLOPS = 2 * (K * R * J + F * R * J + R * N * O + K * N * O)

F32 = mybir.dt.float32
BF16 = mybir.dt.bfloat16
I32 = mybir.dt.int32
U32 = mybir.dt.uint32
U16 = mybir.dt.uint16
U8 = mybir.dt.uint8
E4M3 = mybir.dt.float8_e4m3fn_x4
E5M2 = mybir.dt.float8_e5m2_x4
E2M1 = mybir.dt.float4_e2m1fn_x4
ALU = mybir.AluOpType
COPY = mybir.ActivationFunctionType.Copy
ABS = mybir.ActivationFunctionType.Abs

P = 128
PACK = 4
QUAD = 32


def tile_list_tableread_bank_further_plain_kernel(
    tc, xt_words, xt_scales, w_words, w_scales, xo_words, xo_scales, w0_words, w0_scales, tb, st, sa,
    wb_words, wb_scales, ws_words, ws_scales, offs, offs2, offs3, offs4, offs5, out,
):
    nc = tc.nc
    with ExitStack() as ctx:
        sb = ctx.enter_context(tc.tile_pool(name="sb", bufs=1))
        ps = ctx.enter_context(tc.psum_pool(name="ps", bufs=1))

        def tile(name, shape, dtype):
            return sb.tile(shape, dtype, name=name, align_bytes=64)

        def load_list(name, src):
            lst = tile(name, list(src.shape), U16)
            nc.sync.dma_start(lst[:], src)
            return lst

        def load_words(name, src, columns):
            words = tile(name, [P, columns], U32)
            nc.sync.dma_start(words[:].bitcast(I32), src[0].rearrange("p n t -> p (n t)").bitcast(I32))
            return words

        def zeroed(name, shape):
            plane = tile(name, shape, U8)
            nc.vector.memset(plane[:].bitcast(I32), 0)
            return plane

        def load_plane_direct(queue, plane, src):
            rows = src[0].bitcast(I32)
            for q in range(4):
                queue.dma_start(plane[QUAD * q : QUAD * q + 4, :].bitcast(I32), rows[4 * q : 4 * q + 4, :])

        def load_plane_halves(queue, plane, src):
            rows = src[0].bitcast(I32).rearrange("(h q r) n -> q r h n", h=2, q=2)
            for q in range(2):
                queue.dma_start(plane[QUAD * q : QUAD * q + 4, :, :].bitcast(I32), rows[q])

        def lift_upper_half(plane):
            nc.vector.tensor_copy(plane[64:128, 0, :].bitcast(I32), plane[0:64, 1, :].bitcast(I32))

        def load_staged(queue, staged, src):
            queue.dma_start(staged.bitcast(I32), src[0].bitcast(I32).rearrange("(q r) n -> r q n", r=4))

        def spread(plane, staged):
            for q in range(4):
                nc.vector.tensor_copy(plane[QUAD * q : QUAD * q + 4, :].bitcast(I32), staged[:, q, :].bitcast(I32))

        def gather(name, window, lst, n):
            got = tile(name, [P, n], window.dtype)
            nc.vector.tensor_copy(got[:], window[:].indirect(lst[:]))
            return got


        def deal_words(name, words):
            dealt = tile(name, [P, R], U32)
            nc.scalar.copy(dealt[:].rearrange("p (t m) -> p m t", t=PACK), words[:].rearrange("p (m t) -> p m t", t=PACK))
            return dealt

        def deal_scales(name, plane):
            dealt = tile(name, [P, R], U8)
            nc.vector.tensor_copy(dealt[:].rearrange("p (t m) -> p t m", t=PACK), plane.rearrange("p (m t) -> p t m", t=PACK))
            return dealt

        def halves(queue, plane, src):
            rows = src[0].bitcast(I32).rearrange("(h q r) n -> q r h n", h=2, q=2)
            for q in range(2):
                queue.dma_start(plane[QUAD * q : QUAD * q + 4].bitcast(I32), rows[q])

        xt_st = zeroed("xt_st", [64, 2, T])
        xo_st = zeroed("xo_st", [64, 2, Z])
        w_pl = zeroed("w_pl", [P, 2, 2 * R])
        out_pl = zeroed("out_pl", [P, 2, 2 * N])
        xt_w = tile("xt_w", [P, T], U16)
        st_sb = tile("st_sb", [P, PACK], F32)
        sa_sb = tile("sa_sb", [P, PACK], F32)
        tb_rows = tb.rearrange("(p t) v -> t p v", t=PACK)
        tb_sb = [tile(f"tb_sb{t}", [P, V], F32) for t in range(PACK)]

        l1 = load_list("l1", offs)
        nc.sync.dma_start(xt_w[:].bitcast(I32), xt_words[0].bitcast(I32))
        halves(nc.sync, xt_st[:], xt_scales)
        halves(nc.sync, xo_st[:], xo_scales)
        l2 = load_list("l2", offs2)
        xo_w = load_words("xo_w", xo_words, Z)
        w_w = load_words("w_w", w_words, R)
        w0_w = load_words("w0_w", w0_words, R)
        halves(nc.sync, w_pl[:, :, 0:R], w_scales)
        halves(nc.sync, w_pl[:, :, R : 2 * R], w0_scales)
        nc.sync.dma_start(tb_sb[0][:], tb_rows[0])
        l3 = load_list("l3", offs3)
        nc.sync.dma_start(st_sb[:], st.rearrange("(p t) o -> p (t o)", t=PACK))
        nc.sync.dma_start(tb_sb[1][:], tb_rows[1])
        l4 = load_list("l4", offs4)
        nc.sync.dma_start(sa_sb[:], sa.rearrange("(p t) o -> p (t o)", t=PACK))
        l5 = load_list("l5", offs5)
        nc.sync.dma_start(tb_sb[2][:], tb_rows[2])
        halves(nc.sync, out_pl[:, :, 0:N], wb_scales)
        halves(nc.sync, out_pl[:, :, N : 2 * N], ws_scales)
        nc.sync.dma_start(tb_sb[3][:], tb_rows[3])
        ws_w = load_words("ws_w", ws_words, N)
        wb_w = load_words("wb_w", wb_words, N)

        xt_s = tile("xt_s", [P, T], U8)
        xo_s = tile("xo_s", [P, Z], U8)
        for h in range(2):
            for plane, staged in ((xt_s, xt_st), (xo_s, xo_st)):
                nc.vector.tensor_copy(plane[64 * h : 64 * h + 64, :].bitcast(I32), staged[:, h, :].bitcast(I32))
        xt_g = gather("xt_g", xt_w, l1, J)
        xt_gs = gather("xt_gs", xt_s, l1, J)
        xo_gs = gather("xo_gs", xo_s, l2, J)
        xo_g = gather("xo_g", xo_w, l2, J)
        w_dealt = deal_words("w_dealt", w_w)
        w0_dealt = deal_words("w0_dealt", w0_w)
        lift_upper_half(w_pl)
        by_slot = w_pl[:, 0, :].rearrange("p (x m t) -> p t x m", x=2, t=PACK)
        a_ps = [ps.tile([P, J], F32, name=f"a_ps{t}") for t in range(PACK)]
        for t in range(PACK):
            sc = tile(f"sc{t}", [P, 2, P], U8)
            nc.vector.tensor_copy(sc[:], by_slot[:, t])
            cols = slice(P * t, P * (t + 1))
            nc.tensor.matmul_mx(out=a_ps[t][:], lhsT=w_dealt[:, cols].bitcast(E5M2), lhsT_scale=sc[:, 0, :],
                                rhs=xt_g[:].bitcast(E2M1), rhs_scale=xt_gs[:], start=True, stop=False)
            nc.tensor.matmul_mx(out=a_ps[t][:], lhsT=w0_dealt[:, cols].bitcast(E4M3), lhsT_scale=sc[:, 1, :],
                                rhs=xo_g[:].bitcast(E5M2), rhs_scale=xo_gs[:], start=False, stop=True)

        levels = tile("levels", [P, PACK, O], F32)
        diff = tile("diff", [P, PACK, O], F32)
        hid = tile("hid", [P, O, PACK], BF16)
        for t in range(PACK):
            nc.scalar.activation(levels[:, t, :], tb_sb[t][:].indirect(l3[:]), COPY, scale=st_sb[:, t : t + 1])
        picked_first = sb.tile([P, PACK - 1, O], F32, name="picked_first", tag="tb_sb1", align_bytes=64)
        picked_last = sb.tile([P, O], F32, name="picked_last", tag="tb_sb2", align_bytes=64)
        picked = [picked_first[:, t, :] for t in range(PACK - 1)] + [picked_last[:]]
        for t in range(PACK):
            a_sb = tile(f"a_sb{t}", [P, J], F32)
            nc.vector.tensor_copy(a_sb[:], a_ps[t][:])
            nc.scalar.activation(picked[t], a_sb[:].indirect(l4[:]), COPY, scale=sa_sb[:, t : t + 1])

        xt_g5 = gather("xt_g5", xt_w, l5, O)
        xt_gs5 = gather("xt_gs5", xt_s, l5, O)
        lift_upper_half(out_pl)
        out_sc = out_pl[:, 0, :]
        y_ps = [ps.tile([P, O], F32, name=f"y_ps{h}") for h in range(2)]
        for h in range(2):
            nc.tensor.matmul_mx(out=y_ps[h][:], lhsT=ws_w[:, P * h : P * (h + 1)].bitcast(E4M3),
                                lhsT_scale=out_sc[:, N + P * h : N + P * (h + 1)],
                                rhs=xt_g5[:].bitcast(E2M1), rhs_scale=xt_gs5[:], start=True, stop=False)

        nc.vector.tensor_tensor(diff[:, 0 : PACK - 1, :], levels[:, 0 : PACK - 1, :], picked_first[:], ALU.subtract)
        nc.vector.tensor_tensor(diff[:, PACK - 1, :], levels[:, PACK - 1, :], picked_last[:], ALU.subtract)
        woven = diff[:].rearrange("p t o -> p o t")
        half = O // 2
        nc.scalar.activation(hid[:, 0:half, :], woven[:, 0:half, :], ABS)
        nc.vector.scalar_tensor_tensor(hid[:, half:O, :], woven[:, half:O, :], -1.0, woven[:, half:O, :], ALU.mult, ALU.max)

        hid_q = tile("hid_q", [P, O], U32)
        hid_s = tile("hid_s", [P, O], U8)
        nc.vector.quantize_mx(out=hid_q[:].bitcast(E5M2), scales=hid_s[:], in_=hid[:].rearrange("p o t -> p (o t)"))
        y_sb = tile("y_sb", [P, 2, O], F32)
        for h in range(2):
            nc.tensor.matmul_mx(out=y_ps[h][:], lhsT=wb_w[:, P * h : P * (h + 1)].bitcast(E4M3),
                                lhsT_scale=out_sc[:, P * h : P * (h + 1)],
                                rhs=hid_q[:].bitcast(E5M2), rhs_scale=hid_s[:], start=False, stop=True)
        nc.vector.tensor_copy(y_sb[:, 0, :], y_ps[0][:])
        nc.scalar.copy(y_sb[:, 1, :], y_ps[1][:])
        nc.sync.dma_start(out.rearrange("(h p) o -> p h o", h=2), y_sb[:])
